import numpy as np
import ml_dtypes


def mxq(x, axis, fmt="e4m3"):
    dtype, down = {"e4m3": (ml_dtypes.float8_e4m3fn, 7), "e5m2": (ml_dtypes.float8_e5m2, 14)}[fmt]
    v = np.moveaxis(np.asarray(x, np.float32).astype(ml_dtypes.bfloat16).astype(np.float64), axis, -1)
    blocks = v.reshape(v.shape[:-1] + (-1, 32))
    amax = np.abs(blocks).max(-1, keepdims=True)
    byte = np.maximum(np.where(amax > 0, np.frexp(amax)[1] - 1 + 127, 0) - down, 1)
    scale = np.exp2(byte - 127.0)
    codes = (blocks / scale).astype(np.float32).astype(dtype).astype(np.float64)
    return np.moveaxis((codes * scale).reshape(v.shape), -1, axis)


WIDE = False


def mx_kscale(k):
    if not WIDE:
        return np.ones(k)
    levels = np.array([10, -10, 5, -5, 0])
    if k % 512:
        return np.exp2(np.random.permutation(np.resize(levels, k // 32))).repeat(32)
    a = np.empty((k // 512, 16))
    for p in range(k // 512):
        a[p, :8] = np.random.permutation(np.resize(levels, 8))
        for g in range(8):
            far = levels[np.abs(levels - a[p, g]) >= 10]
            a[p, g + 8] = far[np.random.randint(len(far))]
    return np.exp2(a.ravel()).repeat(32)


BF16 = ml_dtypes.bfloat16


def bf(x):
    return np.asarray(x, np.float32).astype(BF16)


def f64(x):
    return np.asarray(x).astype(np.float64)


E2M1 = np.array([0.0, 0.5, 1.0, 1.5, 2.0, 3.0, 4.0, 6.0, -0.0, -0.5, -1.0, -1.5, -2.0, -3.0, -4.0, -6.0])


def pack_weight(w, fmt):
    k, n = w.shape
    w = f64(bf(w)).reshape(k // 32, 32, n)
    amax = np.abs(w).max(1)
    if fmt == "e4m3":
        byte = np.frexp(amax)[1] - 1 + 127 - 7
    else:
        mant, ex = np.frexp(amax / 6.0)
        byte = np.where(mant > 0.5, ex, ex - 1) + 127
    byte = np.clip(np.where(amax > 0, byte, 1), 1, 254)
    scaled = (w * np.exp2(127.0 - byte)[:, None, :]).reshape(k, n).astype(np.float32)
    by_word = np.ascontiguousarray(scaled.reshape(k // 512, 128, 4, n).transpose(0, 1, 3, 2))
    if fmt == "e4m3":
        words = by_word.astype(ml_dtypes.float8_e4m3fn).view(np.uint8)
    else:
        c = by_word.astype(ml_dtypes.float4_e2m1fn).view(np.uint8) & 0xF
        words = c[..., 0::2] | (c[..., 1::2] << 4)
    return np.ascontiguousarray(words), np.ascontiguousarray(byte.astype(np.uint8).reshape(k // 512, 16, n))


def unpack_weight(words, scales, fmt):
    g, p, n, _ = words.shape
    if fmt == "e4m3":
        vals = np.ascontiguousarray(words).view(ml_dtypes.float8_e4m3fn).astype(np.float64)
    else:
        nib = np.empty((g, p, n, 4), np.uint8)
        nib[..., 0::2] = words & 0xF
        nib[..., 1::2] = words >> 4
        vals = E2M1[nib]
    vals = vals * np.repeat(np.exp2(scales.astype(np.float64) - 127.0), 8, axis=1)[..., None]
    return vals.transpose(0, 1, 3, 2).reshape(g * 512, n)
def pack4(w):
    words, scales = pack_weight(w, "e2m1")
    return words.reshape(words.shape[0], 128, -1), scales


def unpack4(words, scales):
    return unpack_weight(words.reshape(words.shape[0], 128, -1, 2), scales, "e2m1")


def planes(Y):
    n, m = Y.shape
    b = f64(bf(Y)).reshape(n // 32, 32, m)
    amax = np.abs(b).max(1)
    byte = np.clip(np.where(amax > 0, np.frexp(amax)[1] - 1 + 127 - 7, 1), 1, 254)
    codes = (b * np.exp2(127.0 - byte)[:, None, :]).reshape(n, m).astype(np.float32).astype(ml_dtypes.float8_e4m3fn).view(np.uint8)
    words = codes.reshape(n // 512, 128, 4, m).transpose(0, 1, 3, 2)
    return np.ascontiguousarray(words), np.ascontiguousarray(byte.astype(np.uint8).reshape(n // 512, 16, m))


I, J, L, E = 512, 1024, 1536, 2048

def setup_inputs():
    s = mx_kscale(J)
    t = mx_kscale(L)
    tau = 10.0 ** np.random.uniform(-1.5, 1.0, I)
    T1 = 10.0 ** np.random.uniform(-0.7, 0.7, J)
    te = 10.0 ** np.random.uniform(-1.5, 0.3, E)
    T2 = 10.0 ** np.random.uniform(-0.3, 0.7, L)
    K1 = (1.0 - 2.0 * np.exp(-tau[:, None] / T1)) * (1.0 + 0.3 * np.random.randn(I, J)) * 1.2 / np.sqrt(J)
    K2 = np.exp(-te[:, None] / T2) * (1.0 + 0.3 * np.random.randn(E, L)) * 1.5 / np.sqrt(L)
    F0_words, F0_scales = pack4(np.random.randn(J, L) * s[:, None] * t)
    return {
        "K1": bf(K1 / s),
        "F0_words": F0_words,
        "F0_scales": F0_scales,
        "D": bf(0.7 * np.random.randn(J, L) * s[:, None] * t),
        "K2": bf(K2 / t),
        "data": bf(np.random.randn(I, E)),
        "offset": bf(0.3 * np.random.randn(I)),
        "w": bf(np.exp(0.8 * np.random.randn(E))),
    }

def reference(K1, F0_words, F0_scales, D, K2, data, offset, w):
    k1 = mxq(f64(K1), 1)
    H = (k1 @ unpack4(F0_words, F0_scales)) + (k1 @ mxq(f64(D), 0))
    Z = mxq(H, 1) @ mxq(f64(K2), 1).T
    y = (Z + f64(offset)[:, None] - f64(data)) * f64(w)
    words, scales = planes(y.T)
    return y, words, scales

@@ -1,0 +1,387 @@
+from contextlib import ExitStack
+
+import concourse.mybir as mybir
+from concourse.masks import make_identity
+
+I, J, L, E = 512, 1024, 1536, 2048
+FLOPS = 2 * (2 * I * J * L) + 2 * I * L * E
+
+F32 = mybir.dt.float32
+BF16 = mybir.dt.bfloat16
+I32 = mybir.dt.int32
+U32 = mybir.dt.uint32
+U8 = mybir.dt.uint8
+FP8X4 = mybir.dt.float8_e4m3fn_x4
+FP4X4 = mybir.dt.float4_e2m1fn_x4
+ALU = mybir.AluOpType
+
+P = 128
+N = 512
+J_PASSES = J // N
+L_PASSES = L // N
+E_CHUNKS = E // N
+STEPS = 2 * E_CHUNKS
+VECTOR_COLUMNS = 288
+
+
+def tile_relaxometry_weighted_residual_k6_kernel(
+    tc, K1, F0_words, F0_scales, D, K2, data, offset, w, out_0, out_1, out_2
+):
+    nc = tc.nc
+
+    with ExitStack() as ctx:
+        keep = ctx.enter_context(tc.tile_pool(name="keep", bufs=1))
+        work = ctx.enter_context(tc.tile_pool(name="work", bufs=1))
+        psum = ctx.enter_context(tc.psum_pool(name="psum", bufs=1))
+        ctx.enter_context(tc.manual_schedule())
+
+        def held(name, shape, dtype):
+            return keep.tile(shape, dtype, name=name, align_bytes=64)
+
+        free_banks = list(range(8))
+
+        def take_bank():
+            b = free_banks[0]
+            free_banks.remove(b)
+            bank = psum.tile([P, N], F32, name="bank%d" % b)
+            return b, bank
+
+        k1_rows = K1.rearrange("(h p s) j -> h s p j", h=2, s=2)
+        k1_raw = [held("k1_raw%d" % t, [P, J], BF16) for t in range(4)]
+        f0_plane = held("f0_plane", [P, J_PASSES, L], U8)
+        f0_codes = [held("f0_codes%d" % c, [P, J_PASSES, 2 * N], U8) for c in range(L_PASSES)]
+        d_raw = {}
+        for c in range(L_PASSES):
+            for g in range(J_PASSES):
+                d_raw[c, g] = held("d_raw%d_%d" % (c, g), [P, 4, N], BF16)
+        k2_raw = [held("k2_raw%d" % k, [P, 2, L], BF16) for k in range(STEPS)]
+        data_sb = [held("data%d" % h, [P, 2, E], BF16) for h in range(2)]
+        w_sb = held("w_sb", [P, E], BF16)
+        off_sb = held("off_sb", [P, 2, 2], BF16)
+        ident = held("ident", [P, P], F32)
+
+        nc.vector.memset(f0_plane[:].rearrange("p g n -> p (g n)").bitcast(I32), 0)
+        make_identity(nc, ident[:])
+
+        def load_k1(t):
+            nc.sync.dma_start(out=k1_raw[t][:], in_=k1_rows[t // 2, t % 2])
+
+        def load_f0(c):
+            src = F0_words.bitcast(I32)[:, :, c * N // 2 : (c + 1) * N // 2]
+            nc.sync.dma_start(out=f0_codes[c][:].bitcast(I32), in_=src.rearrange("g p n -> p g n"))
+
+        def load_d(c, g):
+            src = D[g * N : (g + 1) * N, c * N : (c + 1) * N]
+            nc.sync.dma_start(out=d_raw[c, g][:], in_=src.rearrange("(p t) n -> p t n", t=4))
+
+        def load_k2(k):
+            src = K2[k * 2 * P : (k + 1) * 2 * P, :]
+            nc.sync.dma_start(out=k2_raw[k][:], in_=src.rearrange("(a p) l -> p a l", p=P))
+
+        def load_data(h):
+            src = data[h * 2 * P : (h + 1) * 2 * P, :]
+            nc.sync.dma_start(out=data_sb[h][:], in_=src.rearrange("(p s) e -> p s e", s=2))
+
+        load_k1(0)
+        load_k1(1)
+        for q in range(4):
+            src = F0_scales.bitcast(I32)[:, 4 * q : 4 * q + 4, :]
+            nc.sync.dma_start(
+                out=f0_plane[32 * q : 32 * q + 4, :, :].bitcast(I32), in_=src.rearrange("g r n -> r g n")
+            )
+        load_f0(0)
+        load_k1(2)
+        load_k1(3)
+        load_d(0, 0)
+        load_f0(1)
+        load_d(0, 1)
+        load_d(1, 0)
+        load_d(1, 1)
+        load_d(2, 0)
+        load_d(2, 1)
+        load_f0(2)
+        load_k2(0)
+        load_k2(1)
+        load_k2(2)
+        nc.sync.dma_start(out=off_sb[:], in_=offset.rearrange("(h p s) -> p h s", h=2, s=2))
+        nc.sync.dma_start(out=w_sb[:], in_=w.partition_broadcast(P))
+        load_data(0)
+        load_k2(3)
+        load_data(1)
+        for k in range(4, STEPS):
+            load_k2(k)
+
+        def turn(sources):
+            b, bank = take_bank()
+            for n, src in enumerate(sources):
+                nc.tensor.transpose(bank[:, n * P : (n + 1) * P], src, ident[:])
+            return b, bank
+
+        def drain(turned, order):
+            b, bank = turned
+            staged = work.tile([P, 2 * N], BF16, name="staged", bufs=6, align_bytes=64)
+            nc.scalar.copy(
+                out=staged[:].bitcast(F32).rearrange("p (x y z) -> p x y z", y=order[1], z=2),
+                in_=bank[:].rearrange(order[0], a=2, u=2),
+            )
+            free_banks.append(b)
+            return staged
+
+        SIDE_BY_SIDE = ("p (a u m) -> p a m u", P)
+        WOVEN = ("p (a u m) -> p m a u", 2)
+
+        def quantize(codes, scales, src):
+            nc.vector.quantize_mx(out=codes.bitcast(FP8X4), scales=scales, in_=src)
+
+        def every_second(words, g):
+            return [words[:, 256 * g + u : 256 * (g + 1) : 2] for u in range(2)]
+
+        def halves(sorted_tile):
+            words = sorted_tile[:].bitcast(F32)
+            return [words[:, u * P : (u + 1) * P] for u in range(2)]
+
+        k1_codes = [held("k1_codes%d" % t, [P, 2 * P], U32) for t in range(4)]
+        k1_scales = [held("k1_scales%d" % t, [P, 2 * P], U8) for t in range(4)]
+
+        def prepare_k1(t):
+            words = k1_raw[t][:].bitcast(F32)
+            staged = drain(turn(every_second(words, 0) + every_second(words, 1)), SIDE_BY_SIDE)
+            quantize(k1_codes[t][:], k1_scales[t][:], staged[:])
+
+        d_codes = {}
+        d_scales = {}
+        d_grouped = {}
+
+        def weave_d(c, g, shared):
+            grouped = work.tile([P, N, 4], BF16, name="d_grouped", bufs=3, align_bytes=64)
+            split = VECTOR_COLUMNS if shared else N
+            nc.vector.tensor_copy(
+                out=grouped[:, :split, :].rearrange("p (c i) t -> p c t i", i=4),
+                in_=d_raw[c, g][:, :, :split].rearrange("p t (c i) -> p c t i", i=4),
+            )
+            if shared:
+                nc.scalar.copy(
+                    out=grouped[:, split:, :].rearrange("p (c i) t -> p c t i", i=4),
+                    in_=d_raw[c, g][:, :, split:].rearrange("p t (c i) -> p c t i", i=4),
+                )
+            d_grouped[c, g] = grouped
+
+        def quantize_d(c, g):
+            d_codes[c, g] = held("d_codes%d_%d" % (c, g), [P, N], U32)
+            d_scales[c, g] = held("d_scales%d_%d" % (c, g), [P, N], U8)
+            quantize(d_codes[c, g][:], d_scales[c, g][:], d_grouped[c, g][:].rearrange("p n t -> p (n t)"))
+
+        h_banks = {}
+        h_sorted = {}
+        h_codes = {}
+        h_scales = {}
+
+        def f0_passes(c, t):
+            h_banks[c, t] = take_bank()
+            for g in range(J_PASSES):
+                nc.tensor.matmul_mx(
+                    out=h_banks[c, t][1][:],
+                    lhsT=k1_codes[t][:, g * P : (g + 1) * P].bitcast(FP8X4),
+                    lhsT_scale=k1_scales[t][:, g * P : (g + 1) * P],
+                    rhs=f0_codes[c][:, g, :].bitcast(FP4X4),
+                    rhs_scale=f0_plane[:, g, c * N : (c + 1) * N],
+                    start=(g == 0),
+                    stop=False,
+                )
+
+        def d_pass(c, g, t):
+            nc.tensor.matmul_mx(
+                out=h_banks[c, t][1][:],
+                lhsT=k1_codes[t][:, g * P : (g + 1) * P].bitcast(FP8X4),
+                lhsT_scale=k1_scales[t][:, g * P : (g + 1) * P],
+                rhs=d_codes[c, g][:].bitcast(FP8X4),
+                rhs_scale=d_scales[c, g][:],
+                start=False,
+                stop=(g == J_PASSES - 1),
+            )
+
+        def round_sorted(copy, name, src):
+            dst = work.tile([P, N], BF16, name=name, bufs=6, align_bytes=64)
+            copy(
+                out=dst[:].rearrange("r (u p e) -> r u p e", u=2, e=2),
+                in_=src.rearrange("r (p u e) -> r u p e", u=2, e=2),
+            )
+            return dst
+
+        def round_h(c, t, copy):
+            b, bank = h_banks[c, t]
+            h_sorted[c, t] = round_sorted(copy, "h_sorted", bank[:])
+            free_banks.append(b)
+
+        def turn_h(c, h):
+            return turn(halves(h_sorted[c, 2 * h]) + halves(h_sorted[c, 2 * h + 1]))
+
+        def quantize_h(c, h, staged):
+            h_codes[c, h] = held("h_codes%d_%d" % (c, h), [P, 2 * P], U32)
+            h_scales[c, h] = held("h_scales%d_%d" % (c, h), [P, 2 * P], U8)
+            quantize(h_codes[c, h][:], h_scales[c, h][:], staged[:])
+
+        k2_codes = {}
+        k2_scales = {}
+
+        def turn_k2(k):
+            staged = []
+            for g in range(L_PASSES):
+                sources = []
+                for a in range(2):
+                    sources.extend(every_second(k2_raw[k][:, a, :].bitcast(F32), g))
+                staged.append(drain(turn(sources), SIDE_BY_SIDE))
+            return staged
+
+        def quantize_k2(k, staged):
+            c, half = divmod(k, 2)
+            cols = slice(half * 2 * P, (half + 1) * 2 * P)
+            for g in range(L_PASSES):
+                if half == 0:
+                    k2_codes[c, g] = work.tile([P, N], U32, name="k2_codes", bufs=9, align_bytes=64)
+                    k2_scales[c, g] = work.tile([P, N], U8, name="k2_scales", bufs=9, align_bytes=64)
+                quantize(k2_codes[c, g][:, cols], k2_scales[c, g][:, cols], staged[g][:])
+
+        z_banks = {}
+        y_tiles = {}
+        y_sorted = {}
+        y_plane = held("y_plane", [P, I], U8)
+
+        def z_passes(k):
+            c, h = divmod(k, 2)
+            for s in range(2):
+                z_banks[k, s] = take_bank()
+                for g in range(L_PASSES):
+                    nc.tensor.matmul_mx(
+                        out=z_banks[k, s][1][:],
+                        lhsT=h_codes[g, h][:, s * P : (s + 1) * P].bitcast(FP8X4),
+                        lhsT_scale=h_scales[g, h][:, s * P : (s + 1) * P],
+                        rhs=k2_codes[c, g][:].bitcast(FP8X4),
+                        rhs_scale=k2_scales[c, g][:],
+                        start=(g == 0),
+                        stop=(g == L_PASSES - 1),
+                    )
+
+        def residual(k):
+            c, h = divmod(k, 2)
+            y_tiles[k] = work.tile([P, 2, N], F32, name="y", bufs=3, align_bytes=64)
+            for s in range(2):
+                b, bank = z_banks[k, s]
+                nc.vector.scalar_tensor_tensor(
+                    out=y_tiles[k][:, s, :],
+                    in0=bank[:],
+                    scalar=off_sb[:, h, s : s + 1],
+                    in1=data_sb[h][:, s, c * N : (c + 1) * N],
+                    op0=ALU.add,
+                    op1=ALU.subtract,
+                )
+                free_banks.append(b)
+
+        def weigh(k, s):
+            c = k // 2
+            nc.vector.tensor_tensor(
+                out=y_tiles[k][:, s, :], in0=y_tiles[k][:, s, :], in1=w_sb[:, c * N : (c + 1) * N], op=ALU.mult
+            )
+
+        def store_y(k):
+            c, h = divmod(k, 2)
+            dst = out_0[h * 2 * P : (h + 1) * 2 * P, c * N : (c + 1) * N]
+            nc.sync.dma_start(out=dst.rearrange("(p s) e -> p s e", s=2), in_=y_tiles[k][:])
+
+        def round_y(k):
+            for s in range(2):
+                y_sorted[k, s] = round_sorted(nc.scalar.copy, "y_sorted", y_tiles[k][:, s, :])
+
+        def turn_y(k):
+            return drain(turn(halves(y_sorted[k, 0]) + halves(y_sorted[k, 1])), WOVEN)
+
+        def quantize_y(k, staged):
+            c, h = divmod(k, 2)
+            cols = slice(h * 2 * P, (h + 1) * 2 * P)
+            y_codes = held("y_codes%d" % k, [P, 2 * P], U32)
+            quantize(y_codes[:], y_plane[4 * c :, cols], staged[:])
+            dst = out_1[c].rearrange("p m t -> p (m t)").bitcast(I32)
+            nc.sync.dma_start(out=dst[:, cols], in_=y_codes[:].bitcast(I32))
+
+        for t in range(3):
+            prepare_k1(t)
+        f0_passes(0, 0)
+        prepare_k1(3)
+        for t in range(1, 4):
+            f0_passes(0, t)
+        for t in range(4):
+            f0_passes(1, t)
+
+        for c in range(2):
+            for g in range(J_PASSES):
+                weave_d(c, g, True)
+                quantize_d(c, g)
+        for g in range(J_PASSES):
+            weave_d(2, g, False)
+        for g in range(J_PASSES):
+            quantize_d(2, g)
+
+        for g in range(J_PASSES):
+            for t in range(4):
+                d_pass(0, g, t)
+        for t in range(4):
+            round_h(0, t, nc.scalar.copy)
+        for g in range(J_PASSES):
+            for t in range(4):
+                d_pass(1, g, t)
+
+        turned = [turn_h(0, h) for h in range(2)]
+        for t in range(2):
+            f0_passes(2, t)
+        for g in range(J_PASSES):
+            for t in range(2):
+                d_pass(2, g, t)
+        for t in range(2):
+            round_h(1, t, nc.scalar.copy)
+        staged_h = [drain(turned[h], SIDE_BY_SIDE) for h in range(2)]
+        for t in range(2, 4):
+            round_h(1, t, nc.vector.tensor_copy)
+        for h in range(2):
+            quantize_h(0, h, staged_h[h])
+
+        for k in range(2):
+            staged_one = drain(turn_h(1, k), SIDE_BY_SIDE)
+            staged_k2 = turn_k2(k)
+            f0_passes(2, 2 + k)
+            for g in range(J_PASSES):
+                d_pass(2, g, 2 + k)
+            for t in range(2 * k, 2 + k):
+                round_h(2, t, nc.vector.tensor_copy)
+            quantize_h(1, k, staged_one)
+            quantize_k2(k, staged_k2)
+
+        for k in range(STEPS + 2):
+            if k < 2:
+                staged_one = drain(turn_h(2, k), SIDE_BY_SIDE)
+            if k == 0:
+                round_h(2, 3, nc.vector.tensor_copy)
+            if 1 <= k <= STEPS:
+                residual(k - 1)
+                weigh(k - 1, 0)
+            if k < 2:
+                quantize_h(2, k, staged_one)
+            if 1 <= k <= STEPS:
+                weigh(k - 1, 1)
+                store_y(k - 1)
+            if k + 2 < STEPS:
+                staged_k2 = turn_k2(k + 2)
+            if k >= 2:
+                staged_one = turn_y(k - 2)
+            if 1 <= k <= STEPS:
+                round_y(k - 1)
+            if k + 2 < STEPS:
+                quantize_k2(k + 2, staged_k2)
+            if k >= 2:
+                quantize_y(k - 2, staged_one)
+            if k < STEPS:
+                z_passes(k)
+
+        for q in range(4):
+            nc.sync.dma_start(
+                out=out_2.bitcast(I32)[:, 4 * q : 4 * q + 4, :], in_=y_plane[32 * q : 32 * q + 16, :].bitcast(I32)
+            )

@@ -17,11 +17,12 @@ ALU = mybir.AluOpType
 
 P = 128
 N = 512
+W = 256
 J_PASSES = J // N
 L_PASSES = L // N
 E_CHUNKS = E // N
 STEPS = 2 * E_CHUNKS
-VECTOR_COLUMNS = 288
+VECTOR_COLUMNS = 272
 
 
 def tile_relaxometry_weighted_residual_k6_kernel(
@@ -48,19 +49,23 @@ def tile_relaxometry_weighted_residual_k6_kernel(
 
         k1_rows = K1.rearrange("(h p s) j -> h s p j", h=2, s=2)
         k1_raw = [held("k1_raw%d" % t, [P, J], BF16) for t in range(4)]
-        f0_plane = held("f0_plane", [P, J_PASSES, L], U8)
+        f0_planes = [held("f0_plane0", [P, J_PASSES, N], U8), held("f0_plane1", [P, J_PASSES, 2 * N], U8)]
         f0_codes = [held("f0_codes%d" % c, [P, J_PASSES, 2 * N], U8) for c in range(L_PASSES)]
         d_raw = {}
         for c in range(L_PASSES):
             for g in range(J_PASSES):
                 d_raw[c, g] = held("d_raw%d_%d" % (c, g), [P, 4, N], BF16)
         k2_raw = [held("k2_raw%d" % k, [P, 2, L], BF16) for k in range(STEPS)]
-        data_sb = [held("data%d" % h, [P, 2, E], BF16) for h in range(2)]
-        w_sb = held("w_sb", [P, E], BF16)
+        data_sb = {}
+        for part in range(2):
+            for h in range(2):
+                data_sb[part, h] = held("data%d_%d" % (part, h), [P, 2, E // 2], BF16)
+        w_sb = [held("w_sb%d" % part, [P, E // 2], BF16) for part in range(2)]
         off_sb = held("off_sb", [P, 2, 2], BF16)
         ident = held("ident", [P, P], F32)
 
-        nc.vector.memset(f0_plane[:].rearrange("p g n -> p (g n)").bitcast(I32), 0)
+        for plane in f0_planes:
+            nc.vector.memset(plane[:].rearrange("p g n -> p (g n)").bitcast(I32), 0)
         make_identity(nc, ident[:])
 
         def load_k1(t):
@@ -78,37 +83,44 @@ def tile_relaxometry_weighted_residual_k6_kernel(
             src = K2[k * 2 * P : (k + 1) * 2 * P, :]
             nc.sync.dma_start(out=k2_raw[k][:], in_=src.rearrange("(a p) l -> p a l", p=P))
 
-        def load_data(h):
-            src = data[h * 2 * P : (h + 1) * 2 * P, :]
-            nc.sync.dma_start(out=data_sb[h][:], in_=src.rearrange("(p s) e -> p s e", s=2))
+        def load_epilogue(part):
+            cols = slice(part * E // 2, (part + 1) * E // 2)
+            nc.sync.dma_start(out=w_sb[part][:], in_=w[cols].partition_broadcast(P))
+            for h in range(2):
+                src = data[h * 2 * P : (h + 1) * 2 * P, cols]
+                nc.sync.dma_start(out=data_sb[part, h][:], in_=src.rearrange("(p s) e -> p s e", s=2))
+
+        def load_f0_scales(plane, first, last):
+            cols = slice(first * N // 4, last * N // 4)
+            for q in range(4):
+                src = F0_scales.bitcast(I32)[:, 4 * q : 4 * q + 4, cols]
+                nc.sync.dma_start(
+                    out=plane[32 * q : 32 * q + 4, :, :].bitcast(I32),
+                    in_=src.rearrange("g r n -> r g n"),
+                )
 
         load_k1(0)
         load_k1(1)
-        for q in range(4):
-            src = F0_scales.bitcast(I32)[:, 4 * q : 4 * q + 4, :]
-            nc.sync.dma_start(
-                out=f0_plane[32 * q : 32 * q + 4, :, :].bitcast(I32), in_=src.rearrange("g r n -> r g n")
-            )
-        load_f0(0)
+        load_f0_scales(f0_planes[0], 0, 1)
         load_k1(2)
         load_k1(3)
-        load_d(0, 0)
+        load_f0(0)
+        pieces = [(c, g) for c in range(L_PASSES) for g in range(J_PASSES)]
+        load_d(*pieces[0])
         load_f0(1)
-        load_d(0, 1)
-        load_d(1, 0)
-        load_d(1, 1)
-        load_d(2, 0)
-        load_d(2, 1)
+        load_f0_scales(f0_planes[1], 1, L_PASSES)
+        for c, g in pieces[1:]:
+            load_d(c, g)
         load_f0(2)
         load_k2(0)
         load_k2(1)
         load_k2(2)
         nc.sync.dma_start(out=off_sb[:], in_=offset.rearrange("(h p s) -> p h s", h=2, s=2))
-        nc.sync.dma_start(out=w_sb[:], in_=w.partition_broadcast(P))
-        load_data(0)
+        load_epilogue(0)
         load_k2(3)
-        load_data(1)
-        for k in range(4, STEPS):
+        load_k2(4)
+        load_epilogue(1)
+        for k in range(5, STEPS):
             load_k2(k)
 
         def turn(sources):
@@ -117,10 +129,10 @@ def tile_relaxometry_weighted_residual_k6_kernel(
                 nc.tensor.transpose(bank[:, n * P : (n + 1) * P], src, ident[:])
             return b, bank
 
-        def drain(turned, order):
+        def drain(turned, order, copy=nc.scalar.copy):
             b, bank = turned
-            staged = work.tile([P, 2 * N], BF16, name="staged", bufs=6, align_bytes=64)
-            nc.scalar.copy(
+            staged = work.tile([P, 2 * N], BF16, name="staged", bufs=8, align_bytes=64)
+            copy(
                 out=staged[:].bitcast(F32).rearrange("p (x y z) -> p x y z", y=order[1], z=2),
                 in_=bank[:].rearrange(order[0], a=2, u=2),
             )
@@ -137,7 +149,7 @@ def tile_relaxometry_weighted_residual_k6_kernel(
             return [words[:, 256 * g + u : 256 * (g + 1) : 2] for u in range(2)]
 
         def halves(sorted_tile):
-            words = sorted_tile[:].bitcast(F32)
+            words = sorted_tile.bitcast(F32)
             return [words[:, u * P : (u + 1) * P] for u in range(2)]
 
         k1_codes = [held("k1_codes%d" % t, [P, 2 * P], U32) for t in range(4)]
@@ -184,7 +196,7 @@ def tile_relaxometry_weighted_residual_k6_kernel(
                     lhsT=k1_codes[t][:, g * P : (g + 1) * P].bitcast(FP8X4),
                     lhsT_scale=k1_scales[t][:, g * P : (g + 1) * P],
                     rhs=f0_codes[c][:, g, :].bitcast(FP4X4),
-                    rhs_scale=f0_plane[:, g, c * N : (c + 1) * N],
+                    rhs_scale=f0_planes[0][:, g, :] if c == 0 else f0_planes[1][:, g, (c - 1) * N : c * N],
                     start=(g == 0),
                     stop=False,
                 )
@@ -200,21 +212,17 @@ def tile_relaxometry_weighted_residual_k6_kernel(
                 stop=(g == J_PASSES - 1),
             )
 
-        def round_sorted(copy, name, src):
-            dst = work.tile([P, N], BF16, name=name, bufs=6, align_bytes=64)
-            copy(
-                out=dst[:].rearrange("r (u p e) -> r u p e", u=2, e=2),
-                in_=src.rearrange("r (p u e) -> r u p e", u=2, e=2),
-            )
-            return dst
-
         def round_h(c, t, copy):
             b, bank = h_banks[c, t]
-            h_sorted[c, t] = round_sorted(copy, "h_sorted", bank[:])
+            h_sorted[c, t] = work.tile([P, N], BF16, name="h_sorted", bufs=6, align_bytes=64)
+            copy(
+                out=h_sorted[c, t][:].rearrange("r (u p e) -> r u p e", u=2, e=2),
+                in_=bank[:].rearrange("r (p u e) -> r u p e", u=2, e=2),
+            )
             free_banks.append(b)
 
         def turn_h(c, h):
-            return turn(halves(h_sorted[c, 2 * h]) + halves(h_sorted[c, 2 * h + 1]))
+            return turn(halves(h_sorted[c, 2 * h][:]) + halves(h_sorted[c, 2 * h + 1][:]))
 
         def quantize_h(c, h, staged):
             h_codes[c, h] = held("h_codes%d_%d" % (c, h), [P, 2 * P], U32)
@@ -224,23 +232,28 @@ def tile_relaxometry_weighted_residual_k6_kernel(
         k2_codes = {}
         k2_scales = {}
 
-        def turn_k2(k):
-            staged = []
-            for g in range(L_PASSES):
-                sources = []
-                for a in range(2):
-                    sources.extend(every_second(k2_raw[k][:, a, :].bitcast(F32), g))
-                staged.append(drain(turn(sources), SIDE_BY_SIDE))
-            return staged
+        k2_sorted = {}
 
-        def quantize_k2(k, staged):
-            c, half = divmod(k, 2)
-            cols = slice(half * 2 * P, (half + 1) * 2 * P)
-            for g in range(L_PASSES):
-                if half == 0:
-                    k2_codes[c, g] = work.tile([P, N], U32, name="k2_codes", bufs=9, align_bytes=64)
-                    k2_scales[c, g] = work.tile([P, N], U8, name="k2_scales", bufs=9, align_bytes=64)
-                quantize(k2_codes[c, g][:, cols], k2_scales[c, g][:, cols], staged[g][:])
+        def sort_k2(k, g, copy=nc.vector.tensor_copy):
+            k2_sorted[k, g] = work.tile([P, 2, N], BF16, name="k2_sorted", bufs=6, align_bytes=64)
+            copy(
+                out=k2_sorted[k, g][:].bitcast(F32).rearrange("r a (u p) -> r a u p", u=2),
+                in_=k2_raw[k][:].bitcast(F32)[:, :, g * W : (g + 1) * W].rearrange("r a (p u) -> r a u p", u=2),
+            )
+
+        def turn_k2(k, g):
+            sources = []
+            for a in range(2):
+                if (k, g) in k2_sorted:
+                    sources.extend(halves(k2_sorted[k, g][:, a, :]))
+                else:
+                    sources.extend(every_second(k2_raw[k][:, a, :].bitcast(F32), g))
+            return drain(turn(sources), SIDE_BY_SIDE)
+
+        def quantize_k2(k, g, staged):
+            k2_codes[k, g] = work.tile([P, W], U32, name="k2_codes", bufs=9, align_bytes=64)
+            k2_scales[k, g] = work.tile([P, W], U8, name="k2_scales", bufs=9, align_bytes=64)
+            quantize(k2_codes[k, g][:], k2_scales[k, g][:], staged[:])
 
         z_banks = {}
         y_tiles = {}
@@ -248,78 +261,86 @@ def tile_relaxometry_weighted_residual_k6_kernel(
         y_plane = held("y_plane", [P, I], U8)
 
         def z_passes(k):
-            c, h = divmod(k, 2)
-            for s in range(2):
-                z_banks[k, s] = take_bank()
-                for g in range(L_PASSES):
-                    nc.tensor.matmul_mx(
-                        out=z_banks[k, s][1][:],
-                        lhsT=h_codes[g, h][:, s * P : (s + 1) * P].bitcast(FP8X4),
-                        lhsT_scale=h_scales[g, h][:, s * P : (s + 1) * P],
-                        rhs=k2_codes[c, g][:].bitcast(FP8X4),
-                        rhs_scale=k2_scales[c, g][:],
-                        start=(g == 0),
-                        stop=(g == L_PASSES - 1),
-                    )
+            for h in range(2):
+                z_banks[k, h] = take_bank()
+                for s in range(2):
+                    for g in range(L_PASSES):
+                        nc.tensor.matmul_mx(
+                            out=z_banks[k, h][1][:, s * W : (s + 1) * W],
+                            lhsT=h_codes[g, h][:, s * P : (s + 1) * P].bitcast(FP8X4),
+                            lhsT_scale=h_scales[g, h][:, s * P : (s + 1) * P],
+                            rhs=k2_codes[k, g][:].bitcast(FP8X4),
+                            rhs_scale=k2_scales[k, g][:],
+                            start=(g == 0),
+                            stop=(g == L_PASSES - 1),
+                        )
 
-        def residual(k):
-            c, h = divmod(k, 2)
-            y_tiles[k] = work.tile([P, 2, N], F32, name="y", bufs=3, align_bytes=64)
-            for s in range(2):
-                b, bank = z_banks[k, s]
+        def echo_columns(k):
+            part, place = divmod(k, STEPS // 2)
+            return part, slice(place * W, (place + 1) * W)
+
+        def residual(k, h, slots):
+            part, cols = echo_columns(k)
+            if slots.start == 0:
+                y_tiles[k, h] = work.tile([P, 2, W], F32, name="y", bufs=10, align_bytes=64)
+            b, bank = z_banks[k, h]
+            for s in range(slots.start, slots.stop):
                 nc.vector.scalar_tensor_tensor(
-                    out=y_tiles[k][:, s, :],
-                    in0=bank[:],
+                    out=y_tiles[k, h][:, s, :],
+                    in0=bank[:, s * W : (s + 1) * W],
                     scalar=off_sb[:, h, s : s + 1],
-                    in1=data_sb[h][:, s, c * N : (c + 1) * N],
+                    in1=data_sb[part, h][:, s, cols],
                     op0=ALU.add,
                     op1=ALU.subtract,
                 )
+            if slots.stop == 2:
                 free_banks.append(b)
 
-        def weigh(k, s):
-            c = k // 2
+        def weigh(k, h, slots):
+            part, cols = echo_columns(k)
             nc.vector.tensor_tensor(
-                out=y_tiles[k][:, s, :], in0=y_tiles[k][:, s, :], in1=w_sb[:, c * N : (c + 1) * N], op=ALU.mult
+                out=y_tiles[k, h][:, slots, :],
+                in0=y_tiles[k, h][:, slots, :],
+                in1=w_sb[part][:, cols].unsqueeze(1).to_broadcast([P, slots.stop - slots.start, W]),
+                op=ALU.mult,
+            )
+            if slots.stop == 2:
+                dst = out_0[h * 2 * P : (h + 1) * 2 * P, k * W : (k + 1) * W]
+                nc.sync.dma_start(out=dst.rearrange("(p s) e -> p s e", s=2), in_=y_tiles[k, h][:])
+
+        def round_y(k, h, slots):
+            c, half = divmod(k, 2)
+            if half == 0:
+                y_sorted[c, h] = work.tile([P, 2, N], BF16, name="y_sorted", bufs=4, align_bytes=64)
+            dst = y_sorted[c, h][:].rearrange("r s (u p e) -> r s u p e", u=2, e=2)
+            nc.scalar.copy(
+                out=dst[:, slots, :, half * P // 2 : (half + 1) * P // 2, :],
+                in_=y_tiles[k, h][:, slots, :].rearrange("r s (p u e) -> r s u p e", u=2, e=2),
             )
 
-        def store_y(k):
-            c, h = divmod(k, 2)
-            dst = out_0[h * 2 * P : (h + 1) * 2 * P, c * N : (c + 1) * N]
-            nc.sync.dma_start(out=dst.rearrange("(p s) e -> p s e", s=2), in_=y_tiles[k][:])
+        def turn_y(c, h, copy=nc.scalar.copy):
+            return drain(turn(halves(y_sorted[c, h][:, 0, :]) + halves(y_sorted[c, h][:, 1, :])), WOVEN, copy)
 
-        def round_y(k):
-            for s in range(2):
-                y_sorted[k, s] = round_sorted(nc.scalar.copy, "y_sorted", y_tiles[k][:, s, :])
-
-        def turn_y(k):
-            return drain(turn(halves(y_sorted[k, 0]) + halves(y_sorted[k, 1])), WOVEN)
-
-        def quantize_y(k, staged):
-            c, h = divmod(k, 2)
+        def quantize_y(c, h, staged):
             cols = slice(h * 2 * P, (h + 1) * 2 * P)
-            y_codes = held("y_codes%d" % k, [P, 2 * P], U32)
+            y_codes = held("y_codes%d_%d" % (c, h), [P, 2 * P], U32)
             quantize(y_codes[:], y_plane[4 * c :, cols], staged[:])
             dst = out_1[c].rearrange("p m t -> p (m t)").bitcast(I32)
             nc.sync.dma_start(out=dst[:, cols], in_=y_codes[:].bitcast(I32))
 
-        for t in range(3):
-            prepare_k1(t)
-        f0_passes(0, 0)
-        prepare_k1(3)
-        for t in range(1, 4):
-            f0_passes(0, t)
         for t in range(4):
-            f0_passes(1, t)
-
+            prepare_k1(t)
         for c in range(2):
-            for g in range(J_PASSES):
-                weave_d(c, g, True)
-                quantize_d(c, g)
-        for g in range(J_PASSES):
-            weave_d(2, g, False)
-        for g in range(J_PASSES):
-            quantize_d(2, g)
+            for t in range(4):
+                f0_passes(c, t)
+
+        for n in range(len(pieces) + 1):
+            if n == 1:
+                quantize_d(*pieces[0])
+            if n < len(pieces):
+                weave_d(*pieces[n], n < 5)
+            if n >= 2:
+                quantize_d(*pieces[n - 1])
 
         for g in range(J_PASSES):
             for t in range(4):
@@ -339,49 +360,90 @@ def tile_relaxometry_weighted_residual_k6_kernel(
         for t in range(2):
             round_h(1, t, nc.scalar.copy)
         staged_h = [drain(turned[h], SIDE_BY_SIDE) for h in range(2)]
+        for g in range(3):
+            sort_k2(0, g)
         for t in range(2, 4):
-            round_h(1, t, nc.vector.tensor_copy)
+            round_h(1, t, nc.scalar.copy)
         for h in range(2):
             quantize_h(0, h, staged_h[h])
+        for t in range(2):
+            round_h(2, t, nc.vector.tensor_copy)
 
-        for k in range(2):
-            staged_one = drain(turn_h(1, k), SIDE_BY_SIDE)
-            staged_k2 = turn_k2(k)
-            f0_passes(2, 2 + k)
-            for g in range(J_PASSES):
-                d_pass(2, g, 2 + k)
-            for t in range(2 * k, 2 + k):
-                round_h(2, t, nc.vector.tensor_copy)
-            quantize_h(1, k, staged_one)
-            quantize_k2(k, staged_k2)
+        first = drain(turn_h(1, 0), SIDE_BY_SIDE)
+        staged_k2 = [turn_k2(0, g) for g in range(L_PASSES)]
+        f0_passes(2, 2)
+        for g in range(J_PASSES):
+            d_pass(2, g, 2)
+        for g in range(3):
+            sort_k2(1, g)
+        quantize_h(1, 0, first)
+        for g in range(L_PASSES):
+            quantize_k2(0, g, staged_k2[g])
+        first = drain(turn_h(1, 1), SIDE_BY_SIDE)
+        second = drain(turn_h(2, 0), SIDE_BY_SIDE)
+        f0_passes(2, 3)
+        for g in range(J_PASSES):
+            d_pass(2, g, 3)
+        round_h(2, 2, nc.vector.tensor_copy)
+        quantize_h(1, 1, first)
+        quantize_h(2, 0, second)
+        round_h(2, 3, nc.vector.tensor_copy)
+        for g in range(3):
+            sort_k2(2, g)
 
-        for k in range(STEPS + 2):
-            if k < 2:
-                staged_one = drain(turn_h(2, k), SIDE_BY_SIDE)
-            if k == 0:
-                round_h(2, 3, nc.vector.tensor_copy)
-            if 1 <= k <= STEPS:
-                residual(k - 1)
-                weigh(k - 1, 0)
-            if k < 2:
-                quantize_h(2, k, staged_one)
-            if 1 <= k <= STEPS:
-                weigh(k - 1, 1)
-                store_y(k - 1)
-            if k + 2 < STEPS:
-                staged_k2 = turn_k2(k + 2)
-            if k >= 2:
-                staged_one = turn_y(k - 2)
-            if 1 <= k <= STEPS:
-                round_y(k - 1)
-            if k + 2 < STEPS:
-                quantize_k2(k + 2, staged_k2)
-            if k >= 2:
-                quantize_y(k - 2, staged_one)
-            if k < STEPS:
-                z_passes(k)
+        staged_k2 = [turn_k2(1, g) for g in range(2)]
+        second = drain(turn_h(2, 1), SIDE_BY_SIDE)
+        staged_k2.append(turn_k2(1, 2))
+        for g in range(2):
+            quantize_k2(1, g, staged_k2[g])
+        quantize_h(2, 1, second)
+        quantize_k2(1, 2, staged_k2[2])
+        z_passes(0)
+
+        both = slice(0, 2)
+        pairs = [(c, h) for c in range(E_CHUNKS) for h in range(2)]
+        staged_y = {}
+        last = STEPS - 1
+        for k in range(1, last):
+            residual(k - 1, 0, both)
+            if k >= 4:
+                quantize_y(*pairs[k - 4], staged_y[k - 4])
+            residual(k - 1, 1, both)
+            for h in range(2):
+                weigh(k - 1, h, both)
+            staged_k2 = [turn_k2(k + 1, g) for g in range(L_PASSES)]
+            if k >= 3:
+                staged_y[k - 3] = turn_y(*pairs[k - 3])
+            for h in range(2):
+                round_y(k - 1, h, both)
+            for g in range(L_PASSES):
+                quantize_k2(k + 1, g, staged_k2[g])
+            z_passes(k)
+
+        residual(last - 1, 0, both)
+        quantize_y(*pairs[last - 4], staged_y[last - 4])
+        residual(last - 1, 1, both)
+        for h in range(2):
+            weigh(last - 1, h, both)
+        for n in range(last - 3, last - 1):
+            staged_y[n] = turn_y(*pairs[n])
+        z_passes(last)
+        for h in range(2):
+            round_y(last - 1, h, both)
+        singles = [(h, slice(s, s + 1)) for h in range(2) for s in range(2)]
+        for n in range(len(singles) + 2):
+            if n >= 2:
+                weigh(last, *singles[n - 2])
+                round_y(last, *singles[n - 2])
+            if n < len(singles):
+                residual(last, *singles[n])
+        for n in range(last - 3, last - 1):
+            quantize_y(*pairs[n], staged_y[n])
+        for n in range(last - 1, last + 1):
+            quantize_y(*pairs[n], turn_y(*pairs[n]))
 
         for q in range(4):
-            nc.sync.dma_start(
+            queue = nc.sync if q % 2 == 0 else nc.scalar
+            queue.dma_start(
                 out=out_2.bitcast(I32)[:, 4 * q : 4 * q + 4, :], in_=y_plane[32 * q : 32 * q + 16, :].bitcast(I32)
             )

from contextlib import ExitStack

import concourse.mybir as mybir
from concourse.masks import make_identity

I, J, L, E = 512, 1024, 1536, 2048
FLOPS = 2 * (2 * I * J * L) + 2 * I * L * E

F32 = mybir.dt.float32
BF16 = mybir.dt.bfloat16
I32 = mybir.dt.int32
U32 = mybir.dt.uint32
U8 = mybir.dt.uint8
FP8X4 = mybir.dt.float8_e4m3fn_x4
FP4X4 = mybir.dt.float4_e2m1fn_x4
ALU = mybir.AluOpType

P = 128
N = 512
W = 256
J_PASSES = J // N
L_PASSES = L // N
E_CHUNKS = E // N
STEPS = 2 * E_CHUNKS
VECTOR_COLUMNS = 272


def tile_relaxometry_weighted_residual_k6_kernel(
    tc, K1, F0_words, F0_scales, D, K2, data, offset, w, out_0, out_1, out_2
):
    nc = tc.nc

    with ExitStack() as ctx:
        keep = ctx.enter_context(tc.tile_pool(name="keep", bufs=1))
        work = ctx.enter_context(tc.tile_pool(name="work", bufs=1))
        psum = ctx.enter_context(tc.psum_pool(name="psum", bufs=1))
        ctx.enter_context(tc.manual_schedule())

        def held(name, shape, dtype):
            return keep.tile(shape, dtype, name=name, align_bytes=64)

        free_banks = list(range(8))

        def take_bank():
            b = free_banks[0]
            free_banks.remove(b)
            bank = psum.tile([P, N], F32, name="bank%d" % b)
            return b, bank

        k1_rows = K1.rearrange("(h p s) j -> h s p j", h=2, s=2)
        k1_raw = [held("k1_raw%d" % t, [P, J], BF16) for t in range(4)]
        f0_planes = [held("f0_plane0", [P, J_PASSES, N], U8), held("f0_plane1", [P, J_PASSES, 2 * N], U8)]
        f0_codes = [held("f0_codes%d" % c, [P, J_PASSES, 2 * N], U8) for c in range(L_PASSES)]
        d_raw = {}
        for c in range(L_PASSES):
            for g in range(J_PASSES):
                d_raw[c, g] = held("d_raw%d_%d" % (c, g), [P, 4, N], BF16)
        k2_raw = [held("k2_raw%d" % k, [P, 2, L], BF16) for k in range(STEPS)]
        data_sb = {}
        for part in range(2):
            for h in range(2):
                data_sb[part, h] = held("data%d_%d" % (part, h), [P, 2, E // 2], BF16)
        w_sb = [held("w_sb%d" % part, [P, E // 2], BF16) for part in range(2)]
        off_sb = held("off_sb", [P, 2, 2], BF16)
        ident = held("ident", [P, P], F32)

        for plane in f0_planes:
            nc.vector.memset(plane[:].rearrange("p g n -> p (g n)").bitcast(I32), 0)
        make_identity(nc, ident[:])

        def load_k1(t):
            nc.sync.dma_start(out=k1_raw[t][:], in_=k1_rows[t // 2, t % 2])

        def load_f0(c):
            src = F0_words.bitcast(I32)[:, :, c * N // 2 : (c + 1) * N // 2]
            nc.sync.dma_start(out=f0_codes[c][:].bitcast(I32), in_=src.rearrange("g p n -> p g n"))

        def load_d(c, g):
            src = D[g * N : (g + 1) * N, c * N : (c + 1) * N]
            nc.sync.dma_start(out=d_raw[c, g][:], in_=src.rearrange("(p t) n -> p t n", t=4))

        def load_k2(k):
            src = K2[k * 2 * P : (k + 1) * 2 * P, :]
            nc.sync.dma_start(out=k2_raw[k][:], in_=src.rearrange("(a p) l -> p a l", p=P))

        def load_epilogue(part):
            cols = slice(part * E // 2, (part + 1) * E // 2)
            nc.sync.dma_start(out=w_sb[part][:], in_=w[cols].partition_broadcast(P))
            for h in range(2):
                src = data[h * 2 * P : (h + 1) * 2 * P, cols]
                nc.sync.dma_start(out=data_sb[part, h][:], in_=src.rearrange("(p s) e -> p s e", s=2))

        def load_f0_scales(plane, first, last):
            cols = slice(first * N // 4, last * N // 4)
            for q in range(4):
                src = F0_scales.bitcast(I32)[:, 4 * q : 4 * q + 4, cols]
                nc.sync.dma_start(
                    out=plane[32 * q : 32 * q + 4, :, :].bitcast(I32),
                    in_=src.rearrange("g r n -> r g n"),
                )

        load_k1(0)
        load_k1(1)
        load_f0_scales(f0_planes[0], 0, 1)
        load_k1(2)
        load_k1(3)
        load_f0(0)
        pieces = [(c, g) for c in range(L_PASSES) for g in range(J_PASSES)]
        load_d(*pieces[0])
        load_f0(1)
        load_f0_scales(f0_planes[1], 1, L_PASSES)
        for c, g in pieces[1:]:
            load_d(c, g)
        load_f0(2)
        load_k2(0)
        load_k2(1)
        load_k2(2)
        nc.sync.dma_start(out=off_sb[:], in_=offset.rearrange("(h p s) -> p h s", h=2, s=2))
        load_epilogue(0)
        load_k2(3)
        load_k2(4)
        load_epilogue(1)
        for k in range(5, STEPS):
            load_k2(k)

        def turn(sources):
            b, bank = take_bank()
            for n, src in enumerate(sources):
                nc.tensor.transpose(bank[:, n * P : (n + 1) * P], src, ident[:])
            return b, bank

        def drain(turned, order, copy=nc.scalar.copy):
            b, bank = turned
            staged = work.tile([P, 2 * N], BF16, name="staged", bufs=8, align_bytes=64)
            copy(
                out=staged[:].bitcast(F32).rearrange("p (x y z) -> p x y z", y=order[1], z=2),
                in_=bank[:].rearrange(order[0], a=2, u=2),
            )
            free_banks.append(b)
            return staged

        SIDE_BY_SIDE = ("p (a u m) -> p a m u", P)
        WOVEN = ("p (a u m) -> p m a u", 2)

        def quantize(codes, scales, src):
            nc.vector.quantize_mx(out=codes.bitcast(FP8X4), scales=scales, in_=src)

        def every_second(words, g):
            return [words[:, 256 * g + u : 256 * (g + 1) : 2] for u in range(2)]

        def halves(sorted_tile):
            words = sorted_tile.bitcast(F32)
            return [words[:, u * P : (u + 1) * P] for u in range(2)]

        k1_codes = [held("k1_codes%d" % t, [P, 2 * P], U32) for t in range(4)]
        k1_scales = [held("k1_scales%d" % t, [P, 2 * P], U8) for t in range(4)]

        def prepare_k1(t):
            words = k1_raw[t][:].bitcast(F32)
            staged = drain(turn(every_second(words, 0) + every_second(words, 1)), SIDE_BY_SIDE)
            quantize(k1_codes[t][:], k1_scales[t][:], staged[:])

        d_codes = {}
        d_scales = {}
        d_grouped = {}

        def weave_d(c, g, shared):
            grouped = work.tile([P, N, 4], BF16, name="d_grouped", bufs=3, align_bytes=64)
            split = VECTOR_COLUMNS if shared else N
            nc.vector.tensor_copy(
                out=grouped[:, :split, :].rearrange("p (c i) t -> p c t i", i=4),
                in_=d_raw[c, g][:, :, :split].rearrange("p t (c i) -> p c t i", i=4),
            )
            if shared:
                nc.scalar.copy(
                    out=grouped[:, split:, :].rearrange("p (c i) t -> p c t i", i=4),
                    in_=d_raw[c, g][:, :, split:].rearrange("p t (c i) -> p c t i", i=4),
                )
            d_grouped[c, g] = grouped

        def quantize_d(c, g):
            d_codes[c, g] = held("d_codes%d_%d" % (c, g), [P, N], U32)
            d_scales[c, g] = held("d_scales%d_%d" % (c, g), [P, N], U8)
            quantize(d_codes[c, g][:], d_scales[c, g][:], d_grouped[c, g][:].rearrange("p n t -> p (n t)"))

        h_banks = {}
        h_sorted = {}
        h_codes = {}
        h_scales = {}

        def f0_passes(c, t):
            h_banks[c, t] = take_bank()
            for g in range(J_PASSES):
                nc.tensor.matmul_mx(
                    out=h_banks[c, t][1][:],
                    lhsT=k1_codes[t][:, g * P : (g + 1) * P].bitcast(FP8X4),
                    lhsT_scale=k1_scales[t][:, g * P : (g + 1) * P],
                    rhs=f0_codes[c][:, g, :].bitcast(FP4X4),
                    rhs_scale=f0_planes[0][:, g, :] if c == 0 else f0_planes[1][:, g, (c - 1) * N : c * N],
                    start=(g == 0),
                    stop=False,
                )

        def d_pass(c, g, t):
            nc.tensor.matmul_mx(
                out=h_banks[c, t][1][:],
                lhsT=k1_codes[t][:, g * P : (g + 1) * P].bitcast(FP8X4),
                lhsT_scale=k1_scales[t][:, g * P : (g + 1) * P],
                rhs=d_codes[c, g][:].bitcast(FP8X4),
                rhs_scale=d_scales[c, g][:],
                start=False,
                stop=(g == J_PASSES - 1),
            )

        def round_h(c, t, copy):
            b, bank = h_banks[c, t]
            h_sorted[c, t] = work.tile([P, N], BF16, name="h_sorted", bufs=6, align_bytes=64)
            copy(
                out=h_sorted[c, t][:].rearrange("r (u p e) -> r u p e", u=2, e=2),
                in_=bank[:].rearrange("r (p u e) -> r u p e", u=2, e=2),
            )
            free_banks.append(b)

        def turn_h(c, h):
            return turn(halves(h_sorted[c, 2 * h][:]) + halves(h_sorted[c, 2 * h + 1][:]))

        def quantize_h(c, h, staged):
            h_codes[c, h] = held("h_codes%d_%d" % (c, h), [P, 2 * P], U32)
            h_scales[c, h] = held("h_scales%d_%d" % (c, h), [P, 2 * P], U8)
            quantize(h_codes[c, h][:], h_scales[c, h][:], staged[:])

        k2_codes = {}
        k2_scales = {}

        k2_sorted = {}

        def sort_k2(k, g, copy=nc.vector.tensor_copy):
            k2_sorted[k, g] = work.tile([P, 2, N], BF16, name="k2_sorted", bufs=6, align_bytes=64)
            copy(
                out=k2_sorted[k, g][:].bitcast(F32).rearrange("r a (u p) -> r a u p", u=2),
                in_=k2_raw[k][:].bitcast(F32)[:, :, g * W : (g + 1) * W].rearrange("r a (p u) -> r a u p", u=2),
            )

        def turn_k2(k, g):
            sources = []
            for a in range(2):
                if (k, g) in k2_sorted:
                    sources.extend(halves(k2_sorted[k, g][:, a, :]))
                else:
                    sources.extend(every_second(k2_raw[k][:, a, :].bitcast(F32), g))
            return drain(turn(sources), SIDE_BY_SIDE)

        def quantize_k2(k, g, staged):
            k2_codes[k, g] = work.tile([P, W], U32, name="k2_codes", bufs=9, align_bytes=64)
            k2_scales[k, g] = work.tile([P, W], U8, name="k2_scales", bufs=9, align_bytes=64)
            quantize(k2_codes[k, g][:], k2_scales[k, g][:], staged[:])

        z_banks = {}
        y_tiles = {}
        y_sorted = {}
        y_plane = held("y_plane", [P, I], U8)

        def z_passes(k):
            for h in range(2):
                z_banks[k, h] = take_bank()
                for s in range(2):
                    for g in range(L_PASSES):
                        nc.tensor.matmul_mx(
                            out=z_banks[k, h][1][:, s * W : (s + 1) * W],
                            lhsT=h_codes[g, h][:, s * P : (s + 1) * P].bitcast(FP8X4),
                            lhsT_scale=h_scales[g, h][:, s * P : (s + 1) * P],
                            rhs=k2_codes[k, g][:].bitcast(FP8X4),
                            rhs_scale=k2_scales[k, g][:],
                            start=(g == 0),
                            stop=(g == L_PASSES - 1),
                        )

        def echo_columns(k):
            part, place = divmod(k, STEPS // 2)
            return part, slice(place * W, (place + 1) * W)

        def residual(k, h, slots):
            part, cols = echo_columns(k)
            if slots.start == 0:
                y_tiles[k, h] = work.tile([P, 2, W], F32, name="y", bufs=10, align_bytes=64)
            b, bank = z_banks[k, h]
            for s in range(slots.start, slots.stop):
                nc.vector.scalar_tensor_tensor(
                    out=y_tiles[k, h][:, s, :],
                    in0=bank[:, s * W : (s + 1) * W],
                    scalar=off_sb[:, h, s : s + 1],
                    in1=data_sb[part, h][:, s, cols],
                    op0=ALU.add,
                    op1=ALU.subtract,
                )
            if slots.stop == 2:
                free_banks.append(b)

        def weigh(k, h, slots):
            part, cols = echo_columns(k)
            nc.vector.tensor_tensor(
                out=y_tiles[k, h][:, slots, :],
                in0=y_tiles[k, h][:, slots, :],
                in1=w_sb[part][:, cols].unsqueeze(1).to_broadcast([P, slots.stop - slots.start, W]),
                op=ALU.mult,
            )
            if slots.stop == 2:
                dst = out_0[h * 2 * P : (h + 1) * 2 * P, k * W : (k + 1) * W]
                nc.sync.dma_start(out=dst.rearrange("(p s) e -> p s e", s=2), in_=y_tiles[k, h][:])

        def round_y(k, h, slots):
            c, half = divmod(k, 2)
            if half == 0:
                y_sorted[c, h] = work.tile([P, 2, N], BF16, name="y_sorted", bufs=4, align_bytes=64)
            dst = y_sorted[c, h][:].rearrange("r s (u p e) -> r s u p e", u=2, e=2)
            nc.scalar.copy(
                out=dst[:, slots, :, half * P // 2 : (half + 1) * P // 2, :],
                in_=y_tiles[k, h][:, slots, :].rearrange("r s (p u e) -> r s u p e", u=2, e=2),
            )

        def turn_y(c, h, copy=nc.scalar.copy):
            return drain(turn(halves(y_sorted[c, h][:, 0, :]) + halves(y_sorted[c, h][:, 1, :])), WOVEN, copy)

        def quantize_y(c, h, staged):
            cols = slice(h * 2 * P, (h + 1) * 2 * P)
            y_codes = held("y_codes%d_%d" % (c, h), [P, 2 * P], U32)
            quantize(y_codes[:], y_plane[4 * c :, cols], staged[:])
            dst = out_1[c].rearrange("p m t -> p (m t)").bitcast(I32)
            nc.sync.dma_start(out=dst[:, cols], in_=y_codes[:].bitcast(I32))

        for t in range(4):
            prepare_k1(t)
        for c in range(2):
            for t in range(4):
                f0_passes(c, t)

        for n in range(len(pieces) + 1):
            if n == 1:
                quantize_d(*pieces[0])
            if n < len(pieces):
                weave_d(*pieces[n], n < 5)
            if n >= 2:
                quantize_d(*pieces[n - 1])

        for g in range(J_PASSES):
            for t in range(4):
                d_pass(0, g, t)
        for t in range(4):
            round_h(0, t, nc.scalar.copy)
        for g in range(J_PASSES):
            for t in range(4):
                d_pass(1, g, t)

        turned = [turn_h(0, h) for h in range(2)]
        for t in range(2):
            f0_passes(2, t)
        for g in range(J_PASSES):
            for t in range(2):
                d_pass(2, g, t)
        for t in range(2):
            round_h(1, t, nc.scalar.copy)
        staged_h = [drain(turned[h], SIDE_BY_SIDE) for h in range(2)]
        for g in range(3):
            sort_k2(0, g)
        for t in range(2, 4):
            round_h(1, t, nc.scalar.copy)
        for h in range(2):
            quantize_h(0, h, staged_h[h])
        for t in range(2):
            round_h(2, t, nc.vector.tensor_copy)

        first = drain(turn_h(1, 0), SIDE_BY_SIDE)
        staged_k2 = [turn_k2(0, g) for g in range(L_PASSES)]
        f0_passes(2, 2)
        for g in range(J_PASSES):
            d_pass(2, g, 2)
        for g in range(3):
            sort_k2(1, g)
        quantize_h(1, 0, first)
        for g in range(L_PASSES):
            quantize_k2(0, g, staged_k2[g])
        first = drain(turn_h(1, 1), SIDE_BY_SIDE)
        second = drain(turn_h(2, 0), SIDE_BY_SIDE)
        f0_passes(2, 3)
        for g in range(J_PASSES):
            d_pass(2, g, 3)
        round_h(2, 2, nc.vector.tensor_copy)
        quantize_h(1, 1, first)
        quantize_h(2, 0, second)
        round_h(2, 3, nc.vector.tensor_copy)
        for g in range(3):
            sort_k2(2, g)

        staged_k2 = [turn_k2(1, g) for g in range(2)]
        second = drain(turn_h(2, 1), SIDE_BY_SIDE)
        staged_k2.append(turn_k2(1, 2))
        for g in range(2):
            quantize_k2(1, g, staged_k2[g])
        quantize_h(2, 1, second)
        quantize_k2(1, 2, staged_k2[2])
        z_passes(0)

        both = slice(0, 2)
        pairs = [(c, h) for c in range(E_CHUNKS) for h in range(2)]
        staged_y = {}
        last = STEPS - 1
        for k in range(1, last):
            residual(k - 1, 0, both)
            if k >= 4:
                quantize_y(*pairs[k - 4], staged_y[k - 4])
            residual(k - 1, 1, both)
            for h in range(2):
                weigh(k - 1, h, both)
            staged_k2 = [turn_k2(k + 1, g) for g in range(L_PASSES)]
            if k >= 3:
                staged_y[k - 3] = turn_y(*pairs[k - 3])
            for h in range(2):
                round_y(k - 1, h, both)
            for g in range(L_PASSES):
                quantize_k2(k + 1, g, staged_k2[g])
            z_passes(k)

        residual(last - 1, 0, both)
        quantize_y(*pairs[last - 4], staged_y[last - 4])
        residual(last - 1, 1, both)
        for h in range(2):
            weigh(last - 1, h, both)
        for n in range(last - 3, last - 1):
            staged_y[n] = turn_y(*pairs[n])
        z_passes(last)
        for h in range(2):
            round_y(last - 1, h, both)
        singles = [(h, slice(s, s + 1)) for h in range(2) for s in range(2)]
        for n in range(len(singles) + 2):
            if n >= 2:
                weigh(last, *singles[n - 2])
                round_y(last, *singles[n - 2])
            if n < len(singles):
                residual(last, *singles[n])
        for n in range(last - 3, last - 1):
            quantize_y(*pairs[n], staged_y[n])
        for n in range(last - 1, last + 1):
            quantize_y(*pairs[n], turn_y(*pairs[n]))

        for q in range(4):
            queue = nc.sync if q % 2 == 0 else nc.scalar
            queue.dma_start(
                out=out_2.bitcast(I32)[:, 4 * q : 4 * q + 4, :], in_=y_plane[32 * q : 32 * q + 16, :].bitcast(I32)
            )
